import numpy as np
import ml_dtypes


def mxq(x, axis, fmt="e4m3"):
    dtype, down = {"e4m3": (ml_dtypes.float8_e4m3fn, 7), "e5m2": (ml_dtypes.float8_e5m2, 14)}[fmt]
    v = np.moveaxis(np.asarray(x, np.float32).astype(ml_dtypes.bfloat16).astype(np.float64), axis, -1)
    blocks = v.reshape(v.shape[:-1] + (-1, 32))
    amax = np.abs(blocks).max(-1, keepdims=True)
    byte = np.maximum(np.where(amax > 0, np.frexp(amax)[1] - 1 + 127, 0) - down, 1)
    scale = np.exp2(byte - 127.0)
    codes = (blocks / scale).astype(np.float32).astype(dtype).astype(np.float64)
    return np.moveaxis((codes * scale).reshape(v.shape), -1, axis)


WIDE = False


def mx_kscale(k):
    if not WIDE:
        return np.ones(k)
    levels = np.array([10, -10, 5, -5, 0])
    if k % 512:
        return np.exp2(np.random.permutation(np.resize(levels, k // 32))).repeat(32)
    a = np.empty((k // 512, 16))
    for p in range(k // 512):
        a[p, :8] = np.random.permutation(np.resize(levels, 8))
        for g in range(8):
            far = levels[np.abs(levels - a[p, g]) >= 10]
            a[p, g + 8] = far[np.random.randint(len(far))]
    return np.exp2(a.ravel()).repeat(32)


def f64(x):
    return np.asarray(x).astype(np.float64)


def striped(idx):
    return np.tile(np.asarray(idx).reshape(-1, 16).T, (8, 1)).astype(np.uint16)


def unstriped(offs):
    return offs[:16].T.reshape(-1).astype(np.int64)


E2M1 = np.array([0.0, 0.5, 1.0, 1.5, 2.0, 3.0, 4.0, 6.0, -0.0, -0.5, -1.0, -1.5, -2.0, -3.0, -4.0, -6.0])


def pack_weight(w, fmt):
    k, n = w.shape
    w = f64(np.asarray(w, np.float32).astype(ml_dtypes.bfloat16)).reshape(k // 32, 32, n)
    amax = np.abs(w).max(1)
    if fmt == "e4m3":
        byte = np.frexp(amax)[1] - 1 + 127 - 7
    else:
        mant, ex = np.frexp(amax / 6.0)
        byte = np.where(mant > 0.5, ex, ex - 1) + 127
    byte = np.clip(np.where(amax > 0, byte, 1), 1, 254)
    scaled = (w * np.exp2(127.0 - byte)[:, None, :]).reshape(k, n).astype(np.float32)
    by_word = np.ascontiguousarray(scaled.reshape(k // 512, 128, 4, n).transpose(0, 1, 3, 2))
    if fmt == "e4m3":
        words = by_word.astype(ml_dtypes.float8_e4m3fn).view(np.uint8)
    else:
        c = by_word.astype(ml_dtypes.float4_e2m1fn).view(np.uint8) & 0xF
        words = (c[..., 0::2] | (c[..., 1::2] << 4)).reshape(k // 512, 128, 2 * n)
    return np.ascontiguousarray(words), np.ascontiguousarray(byte.astype(np.uint8).reshape(k // 512, 16, n))


def unpack_weight(words, scales, fmt):
    g, _, n = scales.shape
    words = np.ascontiguousarray(words).reshape(g, 128, n, -1)
    if fmt == "e4m3":
        vals = words.view(ml_dtypes.float8_e4m3fn).astype(np.float64)
    else:
        nib = np.empty((g, 128, n, 4), np.uint8)
        nib[..., 0::2] = words & 0xF
        nib[..., 1::2] = words >> 4
        vals = E2M1[nib]
    vals = vals * np.repeat(np.exp2(scales.astype(np.float64) - 127.0), 8, axis=1)[..., None]
    return vals.transpose(0, 1, 3, 2).reshape(g * 512, n)


def bf(x):
    return np.asarray(x, np.float32).astype(ml_dtypes.bfloat16)


def planes(Y):
    r, m = Y.shape
    b = f64(bf(Y)).reshape(r // 32, 32, m)
    amax = np.abs(b).max(1)
    byte = np.clip(np.where(amax > 0, np.frexp(amax)[1] - 1 + 127 - 7, 1), 1, 254)
    codes = (b * np.exp2(127.0 - byte)[:, None, :]).reshape(r, m).astype(np.float32).astype(ml_dtypes.float8_e4m3fn).view(np.uint8)
    words = codes.reshape(r // 512, 128, 4, m).transpose(0, 1, 3, 2)
    return np.ascontiguousarray(words), np.ascontiguousarray(byte.astype(np.uint8).reshape(r // 512, 16, m))


D, T, I, J, C, Q = 512, 4096, 512, 512, 1024, 512


def setup_inputs():
    n = np.random.standard_normal
    idx = np.random.permutation(T)[:I]
    fd = mx_kscale(D)
    bankp = pack_weight(n((D, T)) / fd[:, None], "e4m3")
    return {
        "query": (n((D, Q)) * 0.6 / np.sqrt(D) * fd[:, None]).astype(np.float32),
        "bank_words": bankp[0],
        "bank_scales": bankp[1],
        "bkey": (n((D, J)) / fd[:, None]).astype(np.float32),
        "tmp": (np.random.uniform(0.7, 1.3, (Q, 1))).astype(np.float32),
        "offs": striped(idx),
    }


def reference(query, bank_words, bank_scales, bkey, tmp, offs):
    idx = unstriped(offs)
    banku = unpack_weight(bank_words, bank_scales, "e4m3")
    queryq = mxq(f64(query), 0, "e4m3")
    bankidxg = banku[:, idx]
    a = queryq.T @ bankidxg
    bkeyq = mxq(f64(bkey), 0, "e4m3")
    b = queryq.T @ bkeyq
    s = np.concatenate([a, b], axis=1)
    x = s * f64(tmp)
    p = np.exp(x - np.max(x, axis=1, keepdims=True))
    y = p / np.sum(p, axis=1, keepdims=True) * 1024.0
    words, scales = planes(y)
    return y, words, scales

@@ -1,0 +1,168 @@
+from contextlib import ExitStack
+
+import concourse.mybir as mybir
+
+D, T, NEG, KEYS, Q = 512, 4096, 512, 512, 512
+C = NEG + KEYS
+P = 128
+PACK = 4
+FLOPS = 2 * D * Q * C
+
+F32 = mybir.dt.float32
+BF16 = mybir.dt.bfloat16
+I32 = mybir.dt.int32
+U32 = mybir.dt.uint32
+U16 = mybir.dt.uint16
+U8 = mybir.dt.uint8
+FP8X4 = mybir.dt.float8_e4m3fn_x4
+ALU = mybir.AluOpType
+ACT = mybir.ActivationFunctionType
+
+Q_SPLIT = 84
+K_SPLIT = 336
+CHUNKS = ((512, 256, 0), (768, 256, 0), (0, 256, 256), (256, 256, 128))
+SCALAR_NORM = (2, 3)
+
+
+def tile_attend_contrastprobs_pl_kernel(tc, query, bank_words, bank_scales, bkey, tmp, offs, out_0, out_1, out_2):
+    nc = tc.nc
+    with ExitStack() as ctx:
+        keep = ctx.enter_context(tc.tile_pool(name="keep", bufs=1))
+        psum = ctx.enter_context(tc.psum_pool(name="psum", bufs=1))
+
+        k_raw = keep.tile([P, PACK, KEYS], F32, name="k_raw", align_bytes=64)
+        nc.sync.dma_start(out=k_raw[:], in_=bkey.rearrange("(p j) c -> p j c", j=PACK))
+        offsets = keep.tile([P, NEG // 16], U16, name="offsets")
+        nc.sync.dma_start(offsets[:], offs)
+
+        scale_pool = keep.tile([P, T], U8, name="scale_pool", align_bytes=64)
+        nc.vector.memset(scale_pool[:].bitcast(I32), 0)
+        nc.scalar.dma_start(out=scale_pool[0:P:8, :].bitcast(I32), in_=bank_scales[0].bitcast(I32))
+
+        temp = keep.tile([P, PACK], F32, name="temp")
+        nc.sync.dma_start(out=temp[:], in_=tmp.rearrange("(p t) o -> p (t o)", t=PACK))
+        q_raw = keep.tile([P, PACK, Q], F32, name="q_raw", align_bytes=64)
+        nc.sync.dma_start(out=q_raw[:], in_=query.rearrange("(p j) q -> p j q", j=PACK))
+        word_pool = keep.tile([P, T], I32, name="word_pool", tag="pool_bytes", align_bytes=64)
+        nc.sync.dma_start(out=word_pool[:], in_=bank_words[0].rearrange("p n r -> p (n r)").bitcast(I32))
+
+        neg_temp = keep.tile([P, PACK], F32, name="neg_temp")
+        nc.scalar.activation(out=neg_temp[:], in_=temp[:], func=ACT.Copy, scale=-1.0)
+
+        picked_scales = keep.tile([P, NEG], U8, name="picked_scales", align_bytes=64)
+        nc.vector.tensor_copy(out=picked_scales[:], in_=scale_pool[:].indirect(offsets[:]))
+        n_scales = keep.tile([P, NEG], U8, name="n_scales", align_bytes=64)
+        nc.vector.memset(n_scales[:].bitcast(I32), 0)
+        for r in range(4):
+            nc.sync.dma_start(out=n_scales[r:P:32, :].bitcast(I32), in_=picked_scales[8 * r:P:32, :].bitcast(I32))
+
+        k_bf = keep.tile([P, KEYS * PACK], BF16, name="k_bf", align_bytes=64)
+        k_dst = k_bf[:].rearrange("p (c i j) -> p c j i", i=4, j=PACK)
+        k_src = k_raw[:].rearrange("p j (c i) -> p c j i", i=4)
+        nc.vector.tensor_copy(out=k_dst[:, :K_SPLIT // 4], in_=k_src[:, :K_SPLIT // 4])
+        nc.scalar.copy(out=k_dst[:, K_SPLIT // 4:], in_=k_src[:, K_SPLIT // 4:])
+        k_codes = keep.tile([P, KEYS], U32, name="k_codes", align_bytes=64)
+        k_scales = keep.tile([P, KEYS], U8, name="k_scales", align_bytes=64)
+        nc.vector.quantize_mx(out=k_codes[:].bitcast(FP8X4), scales=k_scales[:], in_=k_bf[:])
+
+        q_bf = keep.tile([P, Q * PACK], BF16, name="q_bf", align_bytes=64)
+        q_dst = q_bf[:].rearrange("p (t m j) -> p m j t", t=PACK, j=PACK)
+        q_src = q_raw[:].rearrange("p j (m t) -> p m j t", t=PACK)
+        nc.vector.tensor_copy(out=q_dst[:, :Q_SPLIT], in_=q_src[:, :Q_SPLIT])
+        nc.scalar.copy(out=q_dst[:, Q_SPLIT:], in_=q_src[:, Q_SPLIT:])
+        q_codes = keep.tile([P, Q], U32, name="q_codes", align_bytes=64)
+        q_scales = keep.tile([P, Q], U8, name="q_scales", align_bytes=64)
+        for t in range(PACK):
+            cols = slice(P * t, P * (t + 1))
+            nc.vector.quantize_mx(out=q_codes[:, cols].bitcast(FP8X4), scales=q_scales[:, cols],
+                                  in_=q_bf[:, PACK * P * t:PACK * P * (t + 1)])
+
+        def scores(t, codes, scales, name):
+            bank = psum.tile([P, 512], F32, name=name)
+            cols = slice(P * t, P * (t + 1))
+            nc.tensor.matmul_mx(out=bank[:], lhsT=q_codes[:, cols].bitcast(FP8X4), lhsT_scale=q_scales[:, cols],
+                                rhs=codes, rhs_scale=scales, start=True, stop=True)
+            return bank
+
+        def column(name):
+            return keep.tile([P, 1], F32, name=name)
+
+        key_p, key_negmax, key_sum = [], [], []
+
+        def key_half(t, tag):
+            bank = scores(t, k_codes[:].bitcast(FP8X4), k_scales[:], "key_bank%d" % t)
+            negx = keep.tile([P, KEYS], F32, name="key_negx%d" % t, tag=tag, align_bytes=64)
+            negmax = column("key_negmax%d" % t)
+            nc.vector.tensor_scalar(out=negx[:], in0=bank[:], scalar1=neg_temp[:, t:t + 1], scalar2=None,
+                                    op0=ALU.mult, op1=ALU.min, accum_out=negmax[:])
+            p = keep.tile([P, KEYS], F32, name="key_p%d" % t)
+            total = column("key_total%d" % t)
+            nc.scalar.activation(out=p[:], in_=negx[:], func=ACT.Exp, scale=-1.0, bias=negmax[:], accum_out=total[:])
+            small = column("key_sum%d" % t)
+            nc.scalar.activation(out=small[:], in_=total[:], func=ACT.Copy, scale=1.0 / 1024.0)
+            key_p.append(p)
+            key_negmax.append(negmax)
+            key_sum.append(small)
+
+        for t in range(PACK - 1):
+            key_half(t, "key_negx%d" % t)
+        n_codes = keep.tile([P, NEG], U32, name="n_codes", align_bytes=64)
+        nc.vector.tensor_copy(out=n_codes[:], in_=word_pool[:].bitcast(U32).indirect(offsets[:]))
+        key_half(PACK - 1, "pool_bytes")
+
+        neg_p, shifts, norms = [], [], []
+        for t in range(PACK):
+            bank = scores(t, n_codes[:].bitcast(FP8X4), n_scales[:], "neg_bank%d" % t)
+            negx = keep.tile([P, NEG], F32, name="neg_negx%d" % t)
+            negmax = column("negmax%d" % t)
+            nc.vector.tensor_scalar(out=negx[:], in0=bank[:], scalar1=neg_temp[:, t:t + 1], scalar2=key_negmax[t][:],
+                                    op0=ALU.mult, op1=ALU.min, accum_out=negmax[:])
+            shift = column("shift%d" % t)
+            nc.scalar.activation(out=shift[:], in_=key_negmax[t][:], func=ACT.Exp, scale=-1.0, bias=negmax[:])
+            p = keep.tile([P, NEG], F32, name="neg_p%d" % t)
+            neg_total = column("neg_total%d" % t)
+            nc.scalar.activation(out=p[:], in_=negx[:], func=ACT.Exp, scale=-1.0, bias=negmax[:], accum_out=neg_total[:])
+            key_part = column("key_part%d" % t)
+            nc.scalar.activation(out=key_part[:], in_=shift[:], func=ACT.Copy, scale=key_sum[t][:])
+            total = column("total%d" % t)
+            nc.vector.scalar_tensor_tensor(out=total[:], in0=neg_total[:], scalar=1.0 / 1024.0, in1=key_part[:],
+                                           op0=ALU.mult, op1=ALU.add)
+            norm = column("norm%d" % t)
+            nc.vector.reciprocal(out=norm[:], in_=total[:])
+            neg_p.append(p)
+            shifts.append(shift)
+            norms.append(norm)
+
+        y = keep.tile([P, PACK, C], F32, name="y", align_bytes=64)
+        out_rows = out_0.rearrange("(p t) c -> t p c", t=PACK)
+        for t in range(PACK):
+            nc.vector.tensor_scalar(out=y[:, t, NEG:], in0=key_p[t][:], scalar1=norms[t][:], scalar2=shifts[t][:],
+                                    op0=ALU.mult, op1=ALU.mult)
+            if t == 0:
+                nc.sync.dma_start(out=out_rows[t][:, NEG:], in_=y[:, t, NEG:])
+            if t in SCALAR_NORM:
+                nc.scalar.activation(out=y[:, t, :NEG], in_=neg_p[t][:], func=ACT.Copy, scale=norms[t][:])
+            else:
+                nc.vector.tensor_scalar(out=y[:, t, :NEG], in0=neg_p[t][:], scalar1=norms[t][:], scalar2=None, op0=ALU.mult)
+            done = NEG if t == 0 else C
+            nc.sync.dma_start(out=out_rows[t][:, :done], in_=y[:, t, :done])
+
+        y_codes = keep.tile([P, C], U32, name="y_codes", align_bytes=64)
+        y_scales = keep.tile([P, C], U8, name="y_scales", align_bytes=64)
+        words_out = out_1[0].rearrange("p c r -> p (c r)").bitcast(I32)
+        y_src = y[:].rearrange("p t (c i) -> p c t i", i=4)
+        for c0, width, on_scalar in CHUNKS:
+            y_bf = keep.tile([P, width * PACK], BF16, name="y_bf%d" % c0, align_bytes=64)
+            y_dst = y_bf[:].rearrange("p (c i t) -> p c t i", i=4, t=PACK)
+            cut = on_scalar // 4
+            if on_scalar > 0:
+                nc.scalar.copy(out=y_dst[:, :cut], in_=y_src[:, c0 // 4:c0 // 4 + cut])
+            if on_scalar < width:
+                nc.vector.tensor_copy(out=y_dst[:, cut:], in_=y_src[:, c0 // 4 + cut:(c0 + width) // 4])
+            cols = slice(c0, c0 + width)
+            nc.vector.quantize_mx(out=y_codes[:, cols].bitcast(FP8X4), scales=y_scales[:, cols], in_=y_bf[:])
+            nc.sync.dma_start(out=words_out[:, cols], in_=y_codes[:, cols].bitcast(I32))
+        scales_out = out_2[0].bitcast(I32)
+        for quad in range(4):
+            engine = nc.sync if quad == 3 else nc.scalar
+            engine.dma_start(out=scales_out[4 * quad:4 * quad + 4, :], in_=y_scales[32 * quad:32 * quad + 4, :].bitcast(I32))

@@ -20,7 +20,7 @@ ACT = mybir.ActivationFunctionType
 
 Q_SPLIT = 84
 K_SPLIT = 336
-CHUNKS = ((512, 256, 0), (768, 256, 0), (0, 256, 256), (256, 256, 128))
+CHUNKS = ((512, 256, 0, None), (768, 256, 0, 512), (0, 256, 256, 0), (256, 256, 192, 256))
 SCALAR_NORM = (2, 3)
 
 
@@ -28,8 +28,11 @@ def tile_attend_contrastprobs_pl_kernel(tc, query, bank_words, bank_scales, bkey
     nc = tc.nc
     with ExitStack() as ctx:
         keep = ctx.enter_context(tc.tile_pool(name="keep", bufs=1))
+        placed = ctx.enter_context(tc.tile_pool(name="placed", bufs=1))
         psum = ctx.enter_context(tc.psum_pool(name="psum", bufs=1))
 
+        temp = placed.tile([P, 32], F32, name="temp", offset=4 * T - 64, align_bytes=64)
+        nc.sync.dma_start(out=temp[:, :PACK], in_=tmp.rearrange("(p t) o -> p (t o)", t=PACK))
         k_raw = keep.tile([P, PACK, KEYS], F32, name="k_raw", align_bytes=64)
         nc.sync.dma_start(out=k_raw[:], in_=bkey.rearrange("(p j) c -> p j c", j=PACK))
         offsets = keep.tile([P, NEG // 16], U16, name="offsets")
@@ -39,15 +42,12 @@ def tile_attend_contrastprobs_pl_kernel(tc, query, bank_words, bank_scales, bkey
         nc.vector.memset(scale_pool[:].bitcast(I32), 0)
         nc.scalar.dma_start(out=scale_pool[0:P:8, :].bitcast(I32), in_=bank_scales[0].bitcast(I32))
 
-        temp = keep.tile([P, PACK], F32, name="temp")
-        nc.sync.dma_start(out=temp[:], in_=tmp.rearrange("(p t) o -> p (t o)", t=PACK))
-        q_raw = keep.tile([P, PACK, Q], F32, name="q_raw", align_bytes=64)
-        nc.sync.dma_start(out=q_raw[:], in_=query.rearrange("(p j) q -> p j q", j=PACK))
-        word_pool = keep.tile([P, T], I32, name="word_pool", tag="pool_bytes", align_bytes=64)
-        nc.sync.dma_start(out=word_pool[:], in_=bank_words[0].rearrange("p n r -> p (n r)").bitcast(I32))
-
         neg_temp = keep.tile([P, PACK], F32, name="neg_temp")
-        nc.scalar.activation(out=neg_temp[:], in_=temp[:], func=ACT.Copy, scale=-1.0)
+        nc.vector.tensor_scalar(out=neg_temp[:], in0=temp[:, :PACK], scalar1=-1.0, scalar2=None, op0=ALU.mult)
+        q_raw = placed.tile([P, PACK, Q], F32, name="q_raw", offset=4 * T, align_bytes=64)
+        nc.sync.dma_start(out=q_raw[:], in_=query.rearrange("(p j) q -> p j q", j=PACK))
+        word_pool = placed.tile([P, T], I32, name="word_pool", offset=0, align_bytes=64)
+        nc.sync.dma_start(out=word_pool[:], in_=bank_words[0].rearrange("p n r -> p (n r)").bitcast(I32))
 
         picked_scales = keep.tile([P, NEG], U8, name="picked_scales", align_bytes=64)
         nc.vector.tensor_copy(out=picked_scales[:], in_=scale_pool[:].indirect(offsets[:]))
@@ -60,7 +60,7 @@ def tile_attend_contrastprobs_pl_kernel(tc, query, bank_words, bank_scales, bkey
         k_dst = k_bf[:].rearrange("p (c i j) -> p c j i", i=4, j=PACK)
         k_src = k_raw[:].rearrange("p j (c i) -> p c j i", i=4)
         nc.vector.tensor_copy(out=k_dst[:, :K_SPLIT // 4], in_=k_src[:, :K_SPLIT // 4])
-        nc.scalar.copy(out=k_dst[:, K_SPLIT // 4:], in_=k_src[:, K_SPLIT // 4:])
+        nc.scalar.activation(out=k_dst[:, K_SPLIT // 4:], in_=k_src[:, K_SPLIT // 4:], func=ACT.Copy)
         k_codes = keep.tile([P, KEYS], U32, name="k_codes", align_bytes=64)
         k_scales = keep.tile([P, KEYS], U8, name="k_scales", align_bytes=64)
         nc.vector.quantize_mx(out=k_codes[:].bitcast(FP8X4), scales=k_scales[:], in_=k_bf[:])
@@ -89,9 +89,8 @@ def tile_attend_contrastprobs_pl_kernel(tc, query, bank_words, bank_scales, bkey
 
         key_p, key_negmax, key_sum = [], [], []
 
-        def key_half(t, tag):
+        def key_half(t, negx):
             bank = scores(t, k_codes[:].bitcast(FP8X4), k_scales[:], "key_bank%d" % t)
-            negx = keep.tile([P, KEYS], F32, name="key_negx%d" % t, tag=tag, align_bytes=64)
             negmax = column("key_negmax%d" % t)
             nc.vector.tensor_scalar(out=negx[:], in0=bank[:], scalar1=neg_temp[:, t:t + 1], scalar2=None,
                                     op0=ALU.mult, op1=ALU.min, accum_out=negmax[:])
@@ -105,10 +104,10 @@ def tile_attend_contrastprobs_pl_kernel(tc, query, bank_words, bank_scales, bkey
             key_sum.append(small)
 
         for t in range(PACK - 1):
-            key_half(t, "key_negx%d" % t)
+            key_half(t, keep.tile([P, KEYS], F32, name="key_negx%d" % t))
         n_codes = keep.tile([P, NEG], U32, name="n_codes", align_bytes=64)
         nc.vector.tensor_copy(out=n_codes[:], in_=word_pool[:].bitcast(U32).indirect(offsets[:]))
-        key_half(PACK - 1, "pool_bytes")
+        key_half(PACK - 1, placed.tile([P, KEYS], F32, name="key_negx_last", offset=0, align_bytes=64))
 
         neg_p, shifts, norms = [], [], []
         for t in range(PACK):
@@ -151,7 +150,7 @@ def tile_attend_contrastprobs_pl_kernel(tc, query, bank_words, bank_scales, bkey
         y_scales = keep.tile([P, C], U8, name="y_scales", align_bytes=64)
         words_out = out_1[0].rearrange("p c r -> p (c r)").bitcast(I32)
         y_src = y[:].rearrange("p t (c i) -> p c t i", i=4)
-        for c0, width, on_scalar in CHUNKS:
+        for c0, width, on_scalar, stored in CHUNKS:
             y_bf = keep.tile([P, width * PACK], BF16, name="y_bf%d" % c0, align_bytes=64)
             y_dst = y_bf[:].rearrange("p (c i t) -> p c t i", i=4, t=PACK)
             cut = on_scalar // 4
@@ -161,8 +160,10 @@ def tile_attend_contrastprobs_pl_kernel(tc, query, bank_words, bank_scales, bkey
                 nc.vector.tensor_copy(out=y_dst[:, cut:], in_=y_src[:, c0 // 4 + cut:(c0 + width) // 4])
             cols = slice(c0, c0 + width)
             nc.vector.quantize_mx(out=y_codes[:, cols].bitcast(FP8X4), scales=y_scales[:, cols], in_=y_bf[:])
-            nc.sync.dma_start(out=words_out[:, cols], in_=y_codes[:, cols].bitcast(I32))
+            if stored is not None:
+                span = slice(stored, c0 + width)
+                nc.sync.dma_start(out=words_out[:, span], in_=y_codes[:, span].bitcast(I32))
         scales_out = out_2[0].bitcast(I32)
         for quad in range(4):
-            engine = nc.sync if quad == 3 else nc.scalar
+            engine = nc.sync if quad >= 2 else nc.scalar
             engine.dma_start(out=scales_out[4 * quad:4 * quad + 4, :], in_=y_scales[32 * quad:32 * quad + 4, :].bitcast(I32))

@@ -6,6 +6,7 @@ D, T, NEG, KEYS, Q = 512, 4096, 512, 512, 512
 C = NEG + KEYS
 P = 128
 PACK = 4
+HALF = KEYS // 2
 FLOPS = 2 * D * Q * C
 
 F32 = mybir.dt.float32
@@ -18,8 +19,8 @@ FP8X4 = mybir.dt.float8_e4m3fn_x4
 ALU = mybir.AluOpType
 ACT = mybir.ActivationFunctionType
 
-Q_SPLIT = 84
-K_SPLIT = 336
+Q_SPLIT = 64
+K_SPLIT = (0, 168)
 CHUNKS = ((512, 256, 0, None), (768, 256, 0, 512), (0, 256, 256, 0), (256, 256, 192, 256))
 SCALAR_NORM = (2, 3)
 
@@ -33,8 +34,8 @@ def tile_attend_contrastprobs_pl_kernel(tc, query, bank_words, bank_scales, bkey
 
         temp = placed.tile([P, 32], F32, name="temp", offset=4 * T - 64, align_bytes=64)
         nc.sync.dma_start(out=temp[:, :PACK], in_=tmp.rearrange("(p t) o -> p (t o)", t=PACK))
-        k_raw = keep.tile([P, PACK, KEYS], F32, name="k_raw", align_bytes=64)
-        nc.sync.dma_start(out=k_raw[:], in_=bkey.rearrange("(p j) c -> p j c", j=PACK))
+        q_raw = keep.tile([P, PACK, Q], F32, name="q_raw", align_bytes=64)
+        nc.sync.dma_start(out=q_raw[:], in_=query.rearrange("(p j) q -> p j q", j=PACK))
         offsets = keep.tile([P, NEG // 16], U16, name="offsets")
         nc.sync.dma_start(offsets[:], offs)
 
@@ -44,8 +45,10 @@ def tile_attend_contrastprobs_pl_kernel(tc, query, bank_words, bank_scales, bkey
 
         neg_temp = keep.tile([P, PACK], F32, name="neg_temp")
         nc.vector.tensor_scalar(out=neg_temp[:], in0=temp[:, :PACK], scalar1=-1.0, scalar2=None, op0=ALU.mult)
-        q_raw = placed.tile([P, PACK, Q], F32, name="q_raw", offset=4 * T, align_bytes=64)
-        nc.sync.dma_start(out=q_raw[:], in_=query.rearrange("(p j) q -> p j q", j=PACK))
+        k_raw = placed.tile([P, 2, PACK, HALF], F32, name="k_raw", offset=4 * T, align_bytes=64)
+        key_rows = bkey.rearrange("(p j) (h c) -> h p j c", j=PACK, h=2)
+        for h in range(2):
+            nc.sync.dma_start(out=k_raw[:, h], in_=key_rows[h])
         word_pool = placed.tile([P, T], I32, name="word_pool", offset=0, align_bytes=64)
         nc.sync.dma_start(out=word_pool[:], in_=bank_words[0].rearrange("p n r -> p (n r)").bitcast(I32))
 
@@ -53,35 +56,39 @@ def tile_attend_contrastprobs_pl_kernel(tc, query, bank_words, bank_scales, bkey
         nc.vector.tensor_copy(out=picked_scales[:], in_=scale_pool[:].indirect(offsets[:]))
         n_scales = keep.tile([P, NEG], U8, name="n_scales", align_bytes=64)
         nc.vector.memset(n_scales[:].bitcast(I32), 0)
-        for r in range(4):
-            nc.sync.dma_start(out=n_scales[r:P:32, :].bitcast(I32), in_=picked_scales[8 * r:P:32, :].bitcast(I32))
-
-        k_bf = keep.tile([P, KEYS * PACK], BF16, name="k_bf", align_bytes=64)
-        k_dst = k_bf[:].rearrange("p (c i j) -> p c j i", i=4, j=PACK)
-        k_src = k_raw[:].rearrange("p j (c i) -> p c j i", i=4)
-        nc.vector.tensor_copy(out=k_dst[:, :K_SPLIT // 4], in_=k_src[:, :K_SPLIT // 4])
-        nc.scalar.activation(out=k_dst[:, K_SPLIT // 4:], in_=k_src[:, K_SPLIT // 4:], func=ACT.Copy)
-        k_codes = keep.tile([P, KEYS], U32, name="k_codes", align_bytes=64)
-        k_scales = keep.tile([P, KEYS], U8, name="k_scales", align_bytes=64)
-        nc.vector.quantize_mx(out=k_codes[:].bitcast(FP8X4), scales=k_scales[:], in_=k_bf[:])
 
         q_bf = keep.tile([P, Q * PACK], BF16, name="q_bf", align_bytes=64)
-        q_dst = q_bf[:].rearrange("p (t m j) -> p m j t", t=PACK, j=PACK)
-        q_src = q_raw[:].rearrange("p j (m t) -> p m j t", t=PACK)
+        q_dst = q_bf[:].rearrange("p (t m j) -> p m t j", t=PACK, j=PACK)
+        q_src = q_raw[:].rearrange("p j (m t) -> p m t j", t=PACK)
         nc.vector.tensor_copy(out=q_dst[:, :Q_SPLIT], in_=q_src[:, :Q_SPLIT])
-        nc.scalar.copy(out=q_dst[:, Q_SPLIT:], in_=q_src[:, Q_SPLIT:])
+        nc.scalar.activation(out=q_dst[:, Q_SPLIT:], in_=q_src[:, Q_SPLIT:], func=ACT.Copy)
         q_codes = keep.tile([P, Q], U32, name="q_codes", align_bytes=64)
         q_scales = keep.tile([P, Q], U8, name="q_scales", align_bytes=64)
-        for t in range(PACK):
-            cols = slice(P * t, P * (t + 1))
-            nc.vector.quantize_mx(out=q_codes[:, cols].bitcast(FP8X4), scales=q_scales[:, cols],
-                                  in_=q_bf[:, PACK * P * t:PACK * P * (t + 1)])
+        nc.vector.quantize_mx(out=q_codes[:].bitcast(FP8X4), scales=q_scales[:], in_=q_bf[:])
 
-        def scores(t, codes, scales, name):
+        k_codes = keep.tile([P, KEYS], U32, name="k_codes", align_bytes=64)
+        k_scales = keep.tile([P, KEYS], U8, name="k_scales", align_bytes=64)
+        for h in range(2):
+            k_bf = keep.tile([P, HALF * PACK], BF16, name="k_bf%d" % h, align_bytes=64)
+            k_dst = k_bf[:].rearrange("p (c i j) -> p c j i", i=4, j=PACK)
+            k_src = k_raw[:, h].rearrange("p j (c i) -> p c j i", i=4)
+            cut = K_SPLIT[h] // 4
+            if cut > 0:
+                nc.vector.tensor_copy(out=k_dst[:, :cut], in_=k_src[:, :cut])
+            nc.scalar.copy(out=k_dst[:, cut:], in_=k_src[:, cut:])
+            cols = slice(HALF * h, HALF * (h + 1))
+            nc.vector.quantize_mx(out=k_codes[:, cols].bitcast(FP8X4), scales=k_scales[:, cols], in_=k_bf[:])
+
+        for r in range(4):
+            nc.scalar.dma_start(out=n_scales[r:P:32, :].bitcast(I32), in_=picked_scales[8 * r:P:32, :].bitcast(I32))
+
+        def scores(t, codes, scales, name, width):
             bank = psum.tile([P, 512], F32, name=name)
             cols = slice(P * t, P * (t + 1))
-            nc.tensor.matmul_mx(out=bank[:], lhsT=q_codes[:, cols].bitcast(FP8X4), lhsT_scale=q_scales[:, cols],
-                                rhs=codes, rhs_scale=scales, start=True, stop=True)
+            for n0 in range(0, 512, width):
+                part = slice(n0, n0 + width)
+                nc.tensor.matmul_mx(out=bank[:, part], lhsT=q_codes[:, cols].bitcast(FP8X4), lhsT_scale=q_scales[:, cols],
+                                    rhs=codes[:, part].bitcast(FP8X4), rhs_scale=scales[:, part], start=True, stop=True)
             return bank
 
         def column(name):
@@ -90,7 +97,7 @@ def tile_attend_contrastprobs_pl_kernel(tc, query, bank_words, bank_scales, bkey
         key_p, key_negmax, key_sum = [], [], []
 
         def key_half(t, negx):
-            bank = scores(t, k_codes[:].bitcast(FP8X4), k_scales[:], "key_bank%d" % t)
+            bank = scores(t, k_codes, k_scales, "key_bank%d" % t, HALF)
             negmax = column("key_negmax%d" % t)
             nc.vector.tensor_scalar(out=negx[:], in0=bank[:], scalar1=neg_temp[:, t:t + 1], scalar2=None,
                                     op0=ALU.mult, op1=ALU.min, accum_out=negmax[:])
@@ -111,7 +118,7 @@ def tile_attend_contrastprobs_pl_kernel(tc, query, bank_words, bank_scales, bkey
 
         neg_p, shifts, norms = [], [], []
         for t in range(PACK):
-            bank = scores(t, n_codes[:].bitcast(FP8X4), n_scales[:], "neg_bank%d" % t)
+            bank = scores(t, n_codes, n_scales, "neg_bank%d" % t, NEG)
             negx = keep.tile([P, NEG], F32, name="neg_negx%d" % t)
             negmax = column("negmax%d" % t)
             nc.vector.tensor_scalar(out=negx[:], in0=bank[:], scalar1=neg_temp[:, t:t + 1], scalar2=key_negmax[t][:],

from contextlib import ExitStack

import concourse.mybir as mybir

D, T, NEG, KEYS, Q = 512, 4096, 512, 512, 512
C = NEG + KEYS
P = 128
PACK = 4
HALF = KEYS // 2
FLOPS = 2 * D * Q * C

F32 = mybir.dt.float32
BF16 = mybir.dt.bfloat16
I32 = mybir.dt.int32
U32 = mybir.dt.uint32
U16 = mybir.dt.uint16
U8 = mybir.dt.uint8
FP8X4 = mybir.dt.float8_e4m3fn_x4
ALU = mybir.AluOpType
ACT = mybir.ActivationFunctionType

Q_SPLIT = 64
K_SPLIT = (0, 168)
CHUNKS = ((512, 256, 0, None), (768, 256, 0, 512), (0, 256, 256, 0), (256, 256, 192, 256))
SCALAR_NORM = (2, 3)


def tile_attend_contrastprobs_pl_kernel(tc, query, bank_words, bank_scales, bkey, tmp, offs, out_0, out_1, out_2):
    nc = tc.nc
    with ExitStack() as ctx:
        keep = ctx.enter_context(tc.tile_pool(name="keep", bufs=1))
        placed = ctx.enter_context(tc.tile_pool(name="placed", bufs=1))
        psum = ctx.enter_context(tc.psum_pool(name="psum", bufs=1))

        temp = placed.tile([P, 32], F32, name="temp", offset=4 * T - 64, align_bytes=64)
        nc.sync.dma_start(out=temp[:, :PACK], in_=tmp.rearrange("(p t) o -> p (t o)", t=PACK))
        q_raw = keep.tile([P, PACK, Q], F32, name="q_raw", align_bytes=64)
        nc.sync.dma_start(out=q_raw[:], in_=query.rearrange("(p j) q -> p j q", j=PACK))
        offsets = keep.tile([P, NEG // 16], U16, name="offsets")
        nc.sync.dma_start(offsets[:], offs)

        scale_pool = keep.tile([P, T], U8, name="scale_pool", align_bytes=64)
        nc.vector.memset(scale_pool[:].bitcast(I32), 0)
        nc.scalar.dma_start(out=scale_pool[0:P:8, :].bitcast(I32), in_=bank_scales[0].bitcast(I32))

        neg_temp = keep.tile([P, PACK], F32, name="neg_temp")
        nc.vector.tensor_scalar(out=neg_temp[:], in0=temp[:, :PACK], scalar1=-1.0, scalar2=None, op0=ALU.mult)
        k_raw = placed.tile([P, 2, PACK, HALF], F32, name="k_raw", offset=4 * T, align_bytes=64)
        key_rows = bkey.rearrange("(p j) (h c) -> h p j c", j=PACK, h=2)
        for h in range(2):
            nc.sync.dma_start(out=k_raw[:, h], in_=key_rows[h])
        word_pool = placed.tile([P, T], I32, name="word_pool", offset=0, align_bytes=64)
        nc.sync.dma_start(out=word_pool[:], in_=bank_words[0].rearrange("p n r -> p (n r)").bitcast(I32))

        picked_scales = keep.tile([P, NEG], U8, name="picked_scales", align_bytes=64)
        nc.vector.tensor_copy(out=picked_scales[:], in_=scale_pool[:].indirect(offsets[:]))
        n_scales = keep.tile([P, NEG], U8, name="n_scales", align_bytes=64)
        nc.vector.memset(n_scales[:].bitcast(I32), 0)

        q_bf = keep.tile([P, Q * PACK], BF16, name="q_bf", align_bytes=64)
        q_dst = q_bf[:].rearrange("p (t m j) -> p m t j", t=PACK, j=PACK)
        q_src = q_raw[:].rearrange("p j (m t) -> p m t j", t=PACK)
        nc.vector.tensor_copy(out=q_dst[:, :Q_SPLIT], in_=q_src[:, :Q_SPLIT])
        nc.scalar.activation(out=q_dst[:, Q_SPLIT:], in_=q_src[:, Q_SPLIT:], func=ACT.Copy)
        q_codes = keep.tile([P, Q], U32, name="q_codes", align_bytes=64)
        q_scales = keep.tile([P, Q], U8, name="q_scales", align_bytes=64)
        nc.vector.quantize_mx(out=q_codes[:].bitcast(FP8X4), scales=q_scales[:], in_=q_bf[:])

        k_codes = keep.tile([P, KEYS], U32, name="k_codes", align_bytes=64)
        k_scales = keep.tile([P, KEYS], U8, name="k_scales", align_bytes=64)
        for h in range(2):
            k_bf = keep.tile([P, HALF * PACK], BF16, name="k_bf%d" % h, align_bytes=64)
            k_dst = k_bf[:].rearrange("p (c i j) -> p c j i", i=4, j=PACK)
            k_src = k_raw[:, h].rearrange("p j (c i) -> p c j i", i=4)
            cut = K_SPLIT[h] // 4
            if cut > 0:
                nc.vector.tensor_copy(out=k_dst[:, :cut], in_=k_src[:, :cut])
            nc.scalar.copy(out=k_dst[:, cut:], in_=k_src[:, cut:])
            cols = slice(HALF * h, HALF * (h + 1))
            nc.vector.quantize_mx(out=k_codes[:, cols].bitcast(FP8X4), scales=k_scales[:, cols], in_=k_bf[:])

        for r in range(4):
            nc.scalar.dma_start(out=n_scales[r:P:32, :].bitcast(I32), in_=picked_scales[8 * r:P:32, :].bitcast(I32))

        def scores(t, codes, scales, name, width):
            bank = psum.tile([P, 512], F32, name=name)
            cols = slice(P * t, P * (t + 1))
            for n0 in range(0, 512, width):
                part = slice(n0, n0 + width)
                nc.tensor.matmul_mx(out=bank[:, part], lhsT=q_codes[:, cols].bitcast(FP8X4), lhsT_scale=q_scales[:, cols],
                                    rhs=codes[:, part].bitcast(FP8X4), rhs_scale=scales[:, part], start=True, stop=True)
            return bank

        def column(name):
            return keep.tile([P, 1], F32, name=name)

        key_p, key_negmax, key_sum = [], [], []

        def key_half(t, negx):
            bank = scores(t, k_codes, k_scales, "key_bank%d" % t, HALF)
            negmax = column("key_negmax%d" % t)
            nc.vector.tensor_scalar(out=negx[:], in0=bank[:], scalar1=neg_temp[:, t:t + 1], scalar2=None,
                                    op0=ALU.mult, op1=ALU.min, accum_out=negmax[:])
            p = keep.tile([P, KEYS], F32, name="key_p%d" % t)
            total = column("key_total%d" % t)
            nc.scalar.activation(out=p[:], in_=negx[:], func=ACT.Exp, scale=-1.0, bias=negmax[:], accum_out=total[:])
            small = column("key_sum%d" % t)
            nc.scalar.activation(out=small[:], in_=total[:], func=ACT.Copy, scale=1.0 / 1024.0)
            key_p.append(p)
            key_negmax.append(negmax)
            key_sum.append(small)

        for t in range(PACK - 1):
            key_half(t, keep.tile([P, KEYS], F32, name="key_negx%d" % t))
        n_codes = keep.tile([P, NEG], U32, name="n_codes", align_bytes=64)
        nc.vector.tensor_copy(out=n_codes[:], in_=word_pool[:].bitcast(U32).indirect(offsets[:]))
        key_half(PACK - 1, placed.tile([P, KEYS], F32, name="key_negx_last", offset=0, align_bytes=64))

        neg_p, shifts, norms = [], [], []
        for t in range(PACK):
            bank = scores(t, n_codes, n_scales, "neg_bank%d" % t, NEG)
            negx = keep.tile([P, NEG], F32, name="neg_negx%d" % t)
            negmax = column("negmax%d" % t)
            nc.vector.tensor_scalar(out=negx[:], in0=bank[:], scalar1=neg_temp[:, t:t + 1], scalar2=key_negmax[t][:],
                                    op0=ALU.mult, op1=ALU.min, accum_out=negmax[:])
            shift = column("shift%d" % t)
            nc.scalar.activation(out=shift[:], in_=key_negmax[t][:], func=ACT.Exp, scale=-1.0, bias=negmax[:])
            p = keep.tile([P, NEG], F32, name="neg_p%d" % t)
            neg_total = column("neg_total%d" % t)
            nc.scalar.activation(out=p[:], in_=negx[:], func=ACT.Exp, scale=-1.0, bias=negmax[:], accum_out=neg_total[:])
            key_part = column("key_part%d" % t)
            nc.scalar.activation(out=key_part[:], in_=shift[:], func=ACT.Copy, scale=key_sum[t][:])
            total = column("total%d" % t)
            nc.vector.scalar_tensor_tensor(out=total[:], in0=neg_total[:], scalar=1.0 / 1024.0, in1=key_part[:],
                                           op0=ALU.mult, op1=ALU.add)
            norm = column("norm%d" % t)
            nc.vector.reciprocal(out=norm[:], in_=total[:])
            neg_p.append(p)
            shifts.append(shift)
            norms.append(norm)

        y = keep.tile([P, PACK, C], F32, name="y", align_bytes=64)
        out_rows = out_0.rearrange("(p t) c -> t p c", t=PACK)
        for t in range(PACK):
            nc.vector.tensor_scalar(out=y[:, t, NEG:], in0=key_p[t][:], scalar1=norms[t][:], scalar2=shifts[t][:],
                                    op0=ALU.mult, op1=ALU.mult)
            if t == 0:
                nc.sync.dma_start(out=out_rows[t][:, NEG:], in_=y[:, t, NEG:])
            if t in SCALAR_NORM:
                nc.scalar.activation(out=y[:, t, :NEG], in_=neg_p[t][:], func=ACT.Copy, scale=norms[t][:])
            else:
                nc.vector.tensor_scalar(out=y[:, t, :NEG], in0=neg_p[t][:], scalar1=norms[t][:], scalar2=None, op0=ALU.mult)
            done = NEG if t == 0 else C
            nc.sync.dma_start(out=out_rows[t][:, :done], in_=y[:, t, :done])

        y_codes = keep.tile([P, C], U32, name="y_codes", align_bytes=64)
        y_scales = keep.tile([P, C], U8, name="y_scales", align_bytes=64)
        words_out = out_1[0].rearrange("p c r -> p (c r)").bitcast(I32)
        y_src = y[:].rearrange("p t (c i) -> p c t i", i=4)
        for c0, width, on_scalar, stored in CHUNKS:
            y_bf = keep.tile([P, width * PACK], BF16, name="y_bf%d" % c0, align_bytes=64)
            y_dst = y_bf[:].rearrange("p (c i t) -> p c t i", i=4, t=PACK)
            cut = on_scalar // 4
            if on_scalar > 0:
                nc.scalar.copy(out=y_dst[:, :cut], in_=y_src[:, c0 // 4:c0 // 4 + cut])
            if on_scalar < width:
                nc.vector.tensor_copy(out=y_dst[:, cut:], in_=y_src[:, c0 // 4 + cut:(c0 + width) // 4])
            cols = slice(c0, c0 + width)
            nc.vector.quantize_mx(out=y_codes[:, cols].bitcast(FP8X4), scales=y_scales[:, cols], in_=y_bf[:])
            if stored is not None:
                span = slice(stored, c0 + width)
                nc.sync.dma_start(out=words_out[:, span], in_=y_codes[:, span].bitcast(I32))
        scales_out = out_2[0].bitcast(I32)
        for quad in range(4):
            engine = nc.sync if quad >= 2 else nc.scalar
            engine.dma_start(out=scales_out[4 * quad:4 * quad + 4, :], in_=y_scales[32 * quad:32 * quad + 4, :].bitcast(I32))
